import numpy as np, ml_dtypes
CORES = [36,38,116,118,124,126,164,166,244,246,252,254]
N = 12
TK = 32
def silu(z): return z / (1.0 + np.exp(-z))
def setup_inputs(rng):
    return {"x": rng.standard_normal((N, 128, TK), dtype=np.float32).astype(ml_dtypes.bfloat16), "w1": (rng.standard_normal((N, 128, 128), dtype=np.float32) / 8).astype(ml_dtypes.bfloat16), "w3": (rng.standard_normal((N, 128, 128), dtype=np.float32) / 8).astype(ml_dtypes.bfloat16), "w2": (rng.standard_normal((N, 128, 128), dtype=np.float32) / 8).astype(ml_dtypes.bfloat16)}
def setup_inputs_big(rng):
    d = setup_inputs(rng)
    for k in ("x",): d[k] = (d[k].astype(np.float32) * 1024.0).astype(d[k].dtype)
    return d
def setup_inputs_small(rng):
    d = setup_inputs(rng)
    for k in ("x",): d[k] = (d[k].astype(np.float32) * (1 / 1024.0)).astype(d[k].dtype)
    return d
def setup_inputs_apart(rng):
    d = setup_inputs(rng)
    f = (10.0 ** rng.permutation(np.linspace(-1.5, 1.5, N))).astype(np.float32).reshape(N, 1, 1)
    for k in ("x",): d[k] = (d[k].astype(np.float32) * f).astype(d[k].dtype)
    return d
def reference(x, w1, w3, w2):
    X, W1, W3, W2 = x.astype(np.float64), w1.astype(np.float64), w3.astype(np.float64), w2.astype(np.float64)
    y = np.zeros((N, 128, TK))
    for r in range(N):
        for j in range(N):
            y[r] += W2[j].T @ (silu(W1[j].T @ X[r]) * (W3[j].T @ X[r]))
    return {"y": y.astype(ml_dtypes.bfloat16)}

@@ -1,0 +1,266 @@
+from concourse.bass import DstId, RemoteDMATransfer
+from concourse.mybir import AluOpType, ActivationFunctionType
+
+TK = 32
+D = 128
+MAXCH = 4
+NRET = 5
+
+SCRATCH = {
+    "xq": ("sbuf", [128, 4 * TK], "bfloat16"),
+    "xin": ("sbuf", [128, 2 * MAXCH * TK], "bfloat16"),
+    "wa": ("sbuf", [128, 3 * D], "bfloat16"),
+    "wb": ("sbuf", [128, 3 * D], "bfloat16"),
+    "sl": ("sbuf", [128, 2 * TK + MAXCH * 4 * TK], "float32"),
+    "hh": ("sbuf", [128, 2 * TK + MAXCH * 4 * TK], "bfloat16"),
+    "po": ("sbuf", [128, 2 * MAXCH * TK], "bfloat16"),
+    "land": ("sbuf", [128, NRET * TK], "bfloat16"),
+    "acc": ("sbuf", [128, TK], "float32"),
+    "ysb": ("sbuf", [128, TK], "bfloat16"),
+}
+for _i in range(2 + MAXCH):
+    SCRATCH["ps%d" % _i] = ("psum", [128, 512], "float32")
+
+SEMAPHORES = (["xl", "wl", "ws", "xg", "sent", "st", "yp", "ac"]
+              + ["xs%d" % r for r in range(12)] + ["r%d" % q for q in range(NRET)]
+              + ["%s%s" % (a, c) for a in "zsh" for c in ["A", "B"] + list(range(MAXCH))]
+              + ["%s%d" % (a, c) for a in "pc" for c in range(MAXCH)])
+
+
+def _bits(m):
+    return [b for b in range(m.bit_length()) if (m >> b) & 1]
+
+
+def _mask(bits):
+    m = 0
+    for b in bits:
+        m |= 1 << b
+    return m
+
+
+def _plan(cores, topo):
+    rk = {c: i for i, c in enumerate(cores)}
+    chips = {}
+    for c in cores:
+        chips.setdefault((topo.host(c), topo.chip(c)), []).append(c)
+    keys = list(chips)
+    chip_of = {c: k for k in keys for c in chips[k]}
+    planes = []
+    for k in keys:
+        for pl in planes:
+            if topo.same_plane(chips[k][0], chips[pl[0]][0]):
+                pl.append(k)
+                break
+        else:
+            planes.append([k])
+    reach = {c: sum(1 for d in cores if d != c and topo.may_write(c, d)) for c in cores}
+    plain = {k: min(chips[k], key=lambda c: (reach[c], c)) for k in keys}
+    port = {k: [c for c in chips[k] if c != plain[k]][0] for k in keys}
+    sib = {c: [d for d in chips[chip_of[c]] if d != c][0] for c in cores}
+
+    def handler(k, r):
+        return min([h for h in chips[k] if topo.may_write(h, r)], key=lambda h: (reach[h], h))
+
+    cls, wsem, slot = {}, {}, {}
+    calls = {c: [] for c in cores}
+    for pl in planes:
+        cross = [k for k in keys if k not in pl]
+        gather = len(pl) < len(cross)
+        members = [c for k in pl for c in chips[k]]
+        for c in members:
+            slot[c] = members.index(c) if gather else chips[chip_of[c]].index(c)
+        for k in pl:
+            for c in chips[k]:
+                for k2 in keys:
+                    if k2 == k:
+                        continue
+                    h = handler(k2, c)
+                    if k2 in pl:
+                        cls[(h, c)] = 0 if c == port[k] else 1
+                    else:
+                        cls[(h, c)] = 2 if (gather or c != port[k]) else 0
+                    wsem[(h, c)] = "xg" if (gather and k2 not in pl) else "xs%d" % rk[c]
+    src = {h: sorted([r for r in cores if (h, r) in cls], key=lambda r: (cls[(h, r)], rk[r])) for h in cores}
+    blk = {(h, r): src[h].index(r) for h in cores for r in src[h]}
+    for pl in planes:
+        cross = [k for k in keys if k not in pl]
+        gather = len(pl) < len(cross)
+        members = [c for k in pl for c in chips[k]]
+        for i, k in enumerate(pl):
+            a, b = plain[k], port[k]
+            same = {c: [(handler(k2, c), "xin", blk[(handler(k2, c), c)]) for k2 in pl if k2 != k] for c in (a, b)}
+            if gather:
+                others = [port[k2] for k2 in pl if k2 != k]
+                calls[a].append(([], slot[a], 1, [(p, "xq", slot[a]) for p in others] + [(b, "xq", slot[a])] + same[a],
+                                 "xs%d" % rk[a]))
+                calls[b].append(([], slot[b], 1, [(p, "xq", slot[b]) for p in others] + same[b], "xs%d" % rk[b]))
+                n = len(cross) // len(pl)
+                mine = cross[i * n:(i + 1) * n]
+                calls[b].append((["xs%d" % rk[c] for c in members if c != b], 0, len(members),
+                                 [(port[k2], "xin", blk[(port[k2], members[0])]) for k2 in mine], "xg"))
+            else:
+                far = {c: [(handler(k2, c), "xin", blk[(handler(k2, c), c)]) for k2 in cross] for c in (a, b)}
+                calls[a].append(([], slot[a], 1, [(b, "xq", slot[a])], "xs%d" % rk[a]))
+                calls[a].append(([], slot[a], 1, same[a], "xs%d" % rk[a]))
+                calls[b].append(([], slot[b], 1, far[b] + same[b], "xs%d" % rk[b]))
+                calls[b].append((["xs%d" % rk[a]], slot[a], 1, far[a], "xs%d" % rk[a]))
+    rets = {r: sorted([h for h in cores if (h, r) in cls], key=lambda h: (cls[(h, r)], blk[(h, r)], rk[h])) for r in cores}
+    return {"slot": slot, "sib": sib, "calls": calls, "src": src, "cls": cls, "wait": wsem, "rets": rets}
+
+
+def rank_program(g, core, T, topo):
+    if T.rank_of(core) is None:
+        return
+    cores = list(T.cores)
+    P = _plan(cores, topo)
+    S = T.sem
+    sib = P["sib"][core]
+    pe, act, dve, sy = g.tensor, g.scalar, g.vector, g.sync
+    mult, add = AluOpType.mult, AluOpType.add
+    silu = ActivationFunctionType.Silu
+
+    far_mask = topo.mask(core, sib)
+    for d in cores:
+        if d != core and topo.may_write(core, d):
+            far_mask &= topo.mask(core, d)
+    near_mask = topo.mask(core, sib) & ~far_mask
+    fb = _bits(far_mask)
+    NF, NN = len(fb), len(_bits(near_mask))
+
+    def cols(buf, b, n=1):
+        return T[buf][:, b * TK:(b + n) * TK]
+
+    def transfer(src, dests, sem, mask):
+        ids = []
+        for d, _ in dests:
+            rid, pid = topo.addr(d, core)
+            ids.append(DstId(rid=rid, pnc=pid))
+        return RemoteDMATransfer(dst_ids=ids, dma_engine_mask=mask, remote_sem=sem, srcs=[src],
+                                 dsts=[ap for _, ap in dests])
+
+    xown = cols("xq", P["slot"][core])
+    src = P["src"][core]
+    chunks = [src[i:i + 2] for i in range(0, len(src), 2)]
+    late = [max(P["cls"][(core, r)] for r in ch) == 2 for ch in chunks]
+    groups = [[k for k in range(len(chunks)) if late[k] == f] for f in (False, True)]
+    groups = [gr for gr in groups if gr]
+
+    sy.dma_start(xown, T.x[:, :]).then_inc(S.xl, 16)
+    act.dma_start(T.wa[:, 0:D], T.w1[:, :]).then_inc(S.wl, 16)
+    act.dma_start(T.wa[:, D:2 * D], T.w3[:, :]).then_inc(S.wl, 16)
+    sy.dma_start(T.wa[:, 2 * D:3 * D], T.w2[:, :]).then_inc(S.wl, 16)
+
+    def near_call(sender, call):
+        return all(d == P["sib"][sender] for d, _, _ in call[3])
+
+    inc = {}
+    for c in cores:
+        for call in P["calls"][c]:
+            for d, _, _ in call[3]:
+                if d == core:
+                    inc[call[4]] = NN if near_call(c, call) else NF
+
+    sent = 0
+    g.wait_ge(S.xl, 16)
+    first_wait = [i for i, call in enumerate(P["calls"][core]) if call[0]]
+    w_at = first_wait[0] if first_wait else len(P["calls"][core])
+
+    def send_weights():
+        rid, pid = topo.addr(sib, core)
+        g.wait_ge(S.wl, 48)
+        g.remote_dma(out_ap=T.wb[:, :], in_ap=T.wa[:, :], remote_sem=S.ws, local_sem=S.sent, pid=pid, routing_id=rid,
+                     dma_engine_mask=near_mask)
+        return NN
+
+    for i, call in enumerate(P["calls"][core]):
+        if i == w_at:
+            sent += send_weights()
+        waits, b0, nb, dests, sem = call
+        for w in waits:
+            g.wait_ge(S[w], inc[w])
+        m = near_mask if near_call(core, call) else far_mask
+        g.remote_dma_fused([transfer(cols("xq", b0, nb), [(d, cols(buf, b, nb)) for d, buf, b in dests], S[sem], m)],
+                           local_sem=S.sent)
+        sent += len(_bits(m))
+    if w_at == len(P["calls"][core]):
+        sent += send_weights()
+    for k, ch in enumerate(chunks):
+        g.wait_ge(S["c%d" % k], 1)
+        ne = NF // len(ch)
+        trs = []
+        for j, r in enumerate(ch):
+            q = P["rets"][r].index(core)
+            trs.append(transfer(cols("po", 2 * k + j), [(r, cols("land", q))], S["r%d" % q],
+                                _mask(fb[j * ne:(j + 1) * ne])))
+            sent += ne
+        g.remote_dma_fused(trs, local_sem=S.sent)
+    g.wait_ge(S.sent, sent)
+
+    W = {"A": T.wa, "B": T.wb}
+    own_ps = {"A": T.ps0, "B": T.ps1}
+    own_off = {"A": 0, "B": TK}
+
+    pe.wait_ge(S.xl, 16)
+    pe.wait_ge(S.wl, 48)
+    for s in ("A", "B"):
+        if s == "B":
+            pe.wait_ge(S.ws, NN)
+        ps, o = own_ps[s], own_off[s]
+        pe.matmul(ps[:, 0:TK], W[s][:, 0:D], xown, True, True).then_inc(S["z" + s], 1)
+        pe.matmul(ps[:, TK:2 * TK], W[s][:, D:2 * D], xown, True, True).then_inc(S["z" + s], 1)
+        act.wait_ge(S["z" + s], 2)
+        act.activation(T.sl[:, o:o + TK], ps[:, 0:TK], silu).then_inc(S["s" + s], 1)
+        dve.wait_ge(S["z" + s], 2)
+        dve.wait_ge(S["s" + s], 1)
+        dve.tensor_tensor(T.hh[:, o:o + TK], T.sl[:, o:o + TK], ps[:, TK:2 * TK], mult).then_inc(S["h" + s], 1)
+
+    yown = T.ps1[:, 2 * TK:3 * TK]
+
+    def own_w2():
+        pe.wait_ge(S.hA, 1)
+        pe.wait_ge(S.hB, 1)
+        pe.matmul(yown, T.wa[:, 2 * D:3 * D], T.hh[:, 0:TK], True, False).then_inc(S.yp, 1)
+        pe.matmul(yown, T.wb[:, 2 * D:3 * D], T.hh[:, TK:2 * TK], False, True).then_inc(S.yp, 1)
+
+    for gi, gr in enumerate(groups):
+        for k in gr:
+            n = TK * len(chunks[k])
+            ps = T["ps%d" % (2 + k)]
+            o = 2 * TK + k * 4 * TK
+            xk = T.xin[:, 2 * k * TK:2 * k * TK + n]
+            for w in sorted(set(P["wait"][(core, r)] for r in chunks[k])):
+                pe.wait_ge(S[w], inc[w])
+            pe.matmul(ps[:, 0:n], T.wa[:, 0:D], xk, True, True).then_inc(S["z%d" % k], 1)
+            pe.matmul(ps[:, n:2 * n], T.wb[:, 0:D], xk, True, True).then_inc(S["z%d" % k], 1)
+            pe.matmul(ps[:, 2 * n:3 * n], T.wa[:, D:2 * D], xk, True, True).then_inc(S["z%d" % k], 1)
+            pe.matmul(ps[:, 3 * n:4 * n], T.wb[:, D:2 * D], xk, True, True).then_inc(S["z%d" % k], 1)
+            act.wait_ge(S["z%d" % k], 4)
+            act.activation(T.sl[:, o:o + 2 * n], ps[:, 0:2 * n], silu).then_inc(S["s%d" % k], 1)
+            dve.wait_ge(S["z%d" % k], 4)
+            dve.wait_ge(S["s%d" % k], 1)
+            dve.tensor_tensor(T.hh[:, o:o + 2 * n], T.sl[:, o:o + 2 * n], ps[:, 2 * n:4 * n], mult).then_inc(S["h%d" % k], 1)
+        if gi == 0:
+            own_w2()
+        for k in gr:
+            n = TK * len(chunks[k])
+            ps = T["ps%d" % (2 + k)]
+            o = 2 * TK + k * 4 * TK
+            pe.wait_ge(S["h%d" % k], 1)
+            pe.matmul(ps[:, 4 * n:5 * n], T.wa[:, 2 * D:3 * D], T.hh[:, o:o + n], True, False).then_inc(S["p%d" % k], 1)
+            pe.matmul(ps[:, 4 * n:5 * n], T.wb[:, 2 * D:3 * D], T.hh[:, o + n:o + 2 * n], False, True).then_inc(S["p%d" % k], 1)
+            dve.wait_ge(S["p%d" % k], 2)
+            dve.tensor_copy(T.po[:, 2 * k * TK:2 * k * TK + n], ps[:, 4 * n:5 * n]).then_inc(S["c%d" % k], 1)
+
+    rets = P["rets"][core]
+    dve.wait_ge(S.yp, 2)
+    for q, h in enumerate(rets):
+        hs = P["src"][h]
+        hch = [hs[i:i + 2] for i in range(0, len(hs), 2) if core in hs[i:i + 2]][0]
+        dve.wait_ge(S["r%d" % q], NF // len(hch))
+        if q:
+            dve.wait_ge(S.ac, q)
+        dve.tensor_tensor(T.ysb[:, :] if q == len(rets) - 1 else T.acc[:, :], yown if q == 0 else T.acc[:, :],
+                          cols("land", q), add).then_inc(S.ac, 1)
+    sy.wait_ge(S.ac, len(rets))
+    sy.dma_start(T.y[:, :], T.ysb[:, :]).then_inc(S.st, 16)
+    sy.wait_ge(S.st, 16)

@@ -5,9 +5,13 @@ TK = 32
 D = 128
 MAXCH = 4
 NRET = 5
+NHOP = 4
 
 SCRATCH = {
-    "xq": ("sbuf", [128, 4 * TK], "bfloat16"),
+    "xd": ("dram", [128, TK], "bfloat16"),
+    "xh": ("dram", [128, TK], "bfloat16"),
+    "xq": ("sbuf", [128, 2 * TK], "bfloat16"),
+    "xo": ("sbuf", [128, TK], "bfloat16"),
     "xin": ("sbuf", [128, 2 * MAXCH * TK], "bfloat16"),
     "wa": ("sbuf", [128, 3 * D], "bfloat16"),
     "wb": ("sbuf", [128, 3 * D], "bfloat16"),
@@ -21,7 +25,7 @@ SCRATCH = {
 for _i in range(2 + MAXCH):
     SCRATCH["ps%d" % _i] = ("psum", [128, 512], "float32")
 
-SEMAPHORES = (["xl", "wl", "ws", "xg", "sent", "st", "yp", "ac"]
+SEMAPHORES = (["xl", "xm", "wl", "ws", "xg", "sent", "st", "yp", "ac"]
               + ["xs%d" % r for r in range(12)] + ["r%d" % q for q in range(NRET)]
               + ["%s%s" % (a, c) for a in "zsh" for c in ["A", "B"] + list(range(MAXCH))]
               + ["%s%d" % (a, c) for a in "pc" for c in range(MAXCH)])
@@ -61,51 +65,45 @@ def _plan(cores, topo):
     def handler(k, r):
         return min([h for h in chips[k] if topo.may_write(h, r)], key=lambda h: (reach[h], h))
 
-    cls, wsem, slot = {}, {}, {}
+    far_of, same_of = {}, {}
+    for pl in planes:
+        cross = [k for k in keys if k not in pl]
+        for i, k in enumerate(pl):
+            rot = i * len(cross) // len(pl) if len(pl) > len(cross) else 0
+            far_of[k] = cross[rot:] + cross[:rot]
+            same_of[k] = pl[i + 1:] + pl[:i]
+    gath = {k: len(pl) < len(keys) - len(pl) for pl in planes for k in pl}
+    cls, pos, wsem = {}, {}, {}
+    for k in keys:
+        for c in chips[k]:
+            for j, k2 in enumerate(far_of[k] + same_of[k]):
+                h = handler(k2, c)
+                cls[(h, c)] = 0 if (c == port[k] or k2 in same_of[k]) else 2
+                late_g = gath[k] and cls[(h, c)] == 2
+                pos[(h, c)] = 0 if late_g else j
+                wsem[(h, c)] = "xg" if late_g else "xs%d" % rk[c]
+    src = {h: sorted([r for r in cores if (h, r) in cls], key=lambda r: (cls[(h, r)], pos[(h, r)], rk[r])) for h in cores}
+    blk = {(h, r): src[h].index(r) for h in cores for r in src[h]}
     calls = {c: [] for c in cores}
     for pl in planes:
-        cross = [k for k in keys if k not in pl]
-        gather = len(pl) < len(cross)
-        members = [c for k in pl for c in chips[k]]
-        for c in members:
-            slot[c] = members.index(c) if gather else chips[chip_of[c]].index(c)
-        for k in pl:
-            for c in chips[k]:
-                for k2 in keys:
-                    if k2 == k:
-                        continue
-                    h = handler(k2, c)
-                    if k2 in pl:
-                        cls[(h, c)] = 0 if c == port[k] else 1
-                    else:
-                        cls[(h, c)] = 2 if (gather or c != port[k]) else 0
-                    wsem[(h, c)] = "xg" if (gather and k2 not in pl) else "xs%d" % rk[c]
-    src = {h: sorted([r for r in cores if (h, r) in cls], key=lambda r: (cls[(h, r)], rk[r])) for h in cores}
-    blk = {(h, r): src[h].index(r) for h in cores for r in src[h]}
-    for pl in planes:
-        cross = [k for k in keys if k not in pl]
-        gather = len(pl) < len(cross)
-        members = [c for k in pl for c in chips[k]]
+        pls = [plain[k] for k in pl]
         for i, k in enumerate(pl):
             a, b = plain[k], port[k]
-            same = {c: [(handler(k2, c), "xin", blk[(handler(k2, c), c)]) for k2 in pl if k2 != k] for c in (a, b)}
-            if gather:
-                others = [port[k2] for k2 in pl if k2 != k]
-                calls[a].append(([], slot[a], 1, [(p, "xq", slot[a]) for p in others] + [(b, "xq", slot[a])] + same[a],
-                                 "xs%d" % rk[a]))
-                calls[b].append(([], slot[b], 1, [(p, "xq", slot[b]) for p in others] + same[b], "xs%d" % rk[b]))
-                n = len(cross) // len(pl)
-                mine = cross[i * n:(i + 1) * n]
-                calls[b].append((["xs%d" % rk[c] for c in members if c != b], 0, len(members),
-                                 [(port[k2], "xin", blk[(port[k2], members[0])]) for k2 in mine], "xg"))
+            same = {c: [(handler(k2, c), "xin", blk[(handler(k2, c), c)], 1) for k2 in same_of[k]] for c in (a, b)}
+            far = {c: [(handler(k2, c), "xin", blk[(handler(k2, c), c)], 1) for k2 in far_of[k]] for c in (a, b)}
+            calls[b].append(([], "xd", far[b] + same[b], "xs%d" % rk[b], False))
+            if gath[k]:
+                calls[a].append(([], "xd", [(port[k2], "xq", i, 1) for k2 in same_of[k] + [k]], "xs%d" % rk[a], False))
+                n = len(far_of[k]) // len(pl)
+                mine = far_of[k][i * n:(i + 1) * n]
+                calls[b].append((["xs%d" % rk[c] for c in pls], "xq",
+                                 [(handler(k2, a), "xin", blk[(handler(k2, a), pls[0])], len(pls)) for k2 in mine], "xg", False))
             else:
-                far = {c: [(handler(k2, c), "xin", blk[(handler(k2, c), c)]) for k2 in cross] for c in (a, b)}
-                calls[a].append(([], slot[a], 1, [(b, "xq", slot[a])], "xs%d" % rk[a]))
-                calls[a].append(([], slot[a], 1, same[a], "xs%d" % rk[a]))
-                calls[b].append(([], slot[b], 1, far[b] + same[b], "xs%d" % rk[b]))
-                calls[b].append((["xs%d" % rk[a]], slot[a], 1, far[a], "xs%d" % rk[a]))
+                calls[a].append(([], "xd", [(b, "xh", None, 1)], "xs%d" % rk[a], True))
+                calls[b].append((["xs%d" % rk[a]], "xh", far[a], "xs%d" % rk[a], False))
+            calls[a].append(([], "xd", same[a], "xs%d" % rk[a], False))
     rets = {r: sorted([h for h in cores if (h, r) in cls], key=lambda h: (cls[(h, r)], blk[(h, r)], rk[h])) for r in cores}
-    return {"slot": slot, "sib": sib, "calls": calls, "src": src, "cls": cls, "wait": wsem, "rets": rets}
+    return {"sib": sib, "calls": calls, "src": src, "cls": cls, "wait": wsem, "rets": rets}
 
 
 def rank_program(g, core, T, topo):
@@ -126,6 +124,7 @@ def rank_program(g, core, T, topo):
     near_mask = topo.mask(core, sib) & ~far_mask
     fb = _bits(far_mask)
     NF, NN = len(fb), len(_bits(near_mask))
+    hop_mask = _mask(_bits(near_mask)[:NHOP])
 
     def cols(buf, b, n=1):
         return T[buf][:, b * TK:(b + n) * TK]
@@ -138,27 +137,25 @@ def rank_program(g, core, T, topo):
         return RemoteDMATransfer(dst_ids=ids, dma_engine_mask=mask, remote_sem=sem, srcs=[src],
                                  dsts=[ap for _, ap in dests])
 
-    xown = cols("xq", P["slot"][core])
+    xown = T.xo[:, :]
     src = P["src"][core]
     chunks = [src[i:i + 2] for i in range(0, len(src), 2)]
     late = [max(P["cls"][(core, r)] for r in ch) == 2 for ch in chunks]
     groups = [[k for k in range(len(chunks)) if late[k] == f] for f in (False, True)]
     groups = [gr for gr in groups if gr]
 
-    sy.dma_start(xown, T.x[:, :]).then_inc(S.xl, 16)
+    sy.dma_start(T.xd[:, :], T.x[:, :]).then_inc(S.xl, 16)
     act.dma_start(T.wa[:, 0:D], T.w1[:, :]).then_inc(S.wl, 16)
+    sy.dma_start(xown, T.x[:, :]).then_inc(S.xm, 16)
     act.dma_start(T.wa[:, D:2 * D], T.w3[:, :]).then_inc(S.wl, 16)
     sy.dma_start(T.wa[:, 2 * D:3 * D], T.w2[:, :]).then_inc(S.wl, 16)
-
-    def near_call(sender, call):
-        return all(d == P["sib"][sender] for d, _, _ in call[3])
 
     inc = {}
     for c in cores:
         for call in P["calls"][c]:
-            for d, _, _ in call[3]:
+            for d, _, _, _ in call[2]:
                 if d == core:
-                    inc[call[4]] = NN if near_call(c, call) else NF
+                    inc[call[3]] = NHOP if call[4] else NF
 
     sent = 0
     g.wait_ge(S.xl, 16)
@@ -175,12 +172,12 @@ def rank_program(g, core, T, topo):
     for i, call in enumerate(P["calls"][core]):
         if i == w_at:
             sent += send_weights()
-        waits, b0, nb, dests, sem = call
+        waits, sbuf, dests, sem, hop = call
         for w in waits:
             g.wait_ge(S[w], inc[w])
-        m = near_mask if near_call(core, call) else far_mask
-        g.remote_dma_fused([transfer(cols("xq", b0, nb), [(d, cols(buf, b, nb)) for d, buf, b in dests], S[sem], m)],
-                           local_sem=S.sent)
+        m = hop_mask if hop else far_mask
+        g.remote_dma_fused([transfer(T[sbuf][:, :], [(d, T[buf][:, :] if b is None else cols(buf, b, n)) for d, buf, b, n in dests],
+                                     S[sem], m)], local_sem=S.sent)
         sent += len(_bits(m))
     if w_at == len(P["calls"][core]):
         sent += send_weights()
@@ -200,7 +197,7 @@ def rank_program(g, core, T, topo):
     own_ps = {"A": T.ps0, "B": T.ps1}
     own_off = {"A": 0, "B": TK}
 
-    pe.wait_ge(S.xl, 16)
+    pe.wait_ge(S.xm, 16)
     pe.wait_ge(S.wl, 48)
     for s in ("A", "B"):
         if s == "B":
@@ -222,34 +219,41 @@ def rank_program(g, core, T, topo):
         pe.matmul(yown, T.wa[:, 2 * D:3 * D], T.hh[:, 0:TK], True, False).then_inc(S.yp, 1)
         pe.matmul(yown, T.wb[:, 2 * D:3 * D], T.hh[:, TK:2 * TK], False, True).then_inc(S.yp, 1)
 
+    def first_half(k):
+        n = TK * len(chunks[k])
+        ps = T["ps%d" % (2 + k)]
+        o = 2 * TK + k * 4 * TK
+        xk = T.xin[:, 2 * k * TK:2 * k * TK + n]
+        for w in sorted(set(P["wait"][(core, r)] for r in chunks[k])):
+            pe.wait_ge(S[w], inc[w])
+        pe.matmul(ps[:, 0:n], T.wa[:, 0:D], xk, True, True).then_inc(S["z%d" % k], 1)
+        pe.matmul(ps[:, n:2 * n], T.wb[:, 0:D], xk, True, True).then_inc(S["z%d" % k], 1)
+        pe.matmul(ps[:, 2 * n:3 * n], T.wa[:, D:2 * D], xk, True, True).then_inc(S["z%d" % k], 1)
+        pe.matmul(ps[:, 3 * n:4 * n], T.wb[:, D:2 * D], xk, True, True).then_inc(S["z%d" % k], 1)
+        act.wait_ge(S["z%d" % k], 4)
+        act.activation(T.sl[:, o:o + 2 * n], ps[:, 0:2 * n], silu).then_inc(S["s%d" % k], 1)
+        dve.wait_ge(S["z%d" % k], 4)
+        dve.wait_ge(S["s%d" % k], 1)
+        dve.tensor_tensor(T.hh[:, o:o + 2 * n], T.sl[:, o:o + 2 * n], ps[:, 2 * n:4 * n], mult).then_inc(S["h%d" % k], 1)
+
+    def second_half(k):
+        n = TK * len(chunks[k])
+        ps = T["ps%d" % (2 + k)]
+        o = 2 * TK + k * 4 * TK
+        pe.wait_ge(S["h%d" % k], 1)
+        pe.matmul(ps[:, 4 * n:5 * n], T.wa[:, 2 * D:3 * D], T.hh[:, o:o + n], True, False).then_inc(S["p%d" % k], 1)
+        pe.matmul(ps[:, 4 * n:5 * n], T.wb[:, 2 * D:3 * D], T.hh[:, o + n:o + 2 * n], False, True).then_inc(S["p%d" % k], 1)
+        dve.wait_ge(S["p%d" % k], 2)
+        dve.tensor_copy(T.po[:, 2 * k * TK:2 * k * TK + n], ps[:, 4 * n:5 * n]).then_inc(S["c%d" % k], 1)
+
     for gi, gr in enumerate(groups):
-        for k in gr:
-            n = TK * len(chunks[k])
-            ps = T["ps%d" % (2 + k)]
-            o = 2 * TK + k * 4 * TK
-            xk = T.xin[:, 2 * k * TK:2 * k * TK + n]
-            for w in sorted(set(P["wait"][(core, r)] for r in chunks[k])):
-                pe.wait_ge(S[w], inc[w])
-            pe.matmul(ps[:, 0:n], T.wa[:, 0:D], xk, True, True).then_inc(S["z%d" % k], 1)
-            pe.matmul(ps[:, n:2 * n], T.wb[:, 0:D], xk, True, True).then_inc(S["z%d" % k], 1)
-            pe.matmul(ps[:, 2 * n:3 * n], T.wa[:, D:2 * D], xk, True, True).then_inc(S["z%d" % k], 1)
-            pe.matmul(ps[:, 3 * n:4 * n], T.wb[:, D:2 * D], xk, True, True).then_inc(S["z%d" % k], 1)
-            act.wait_ge(S["z%d" % k], 4)
-            act.activation(T.sl[:, o:o + 2 * n], ps[:, 0:2 * n], silu).then_inc(S["s%d" % k], 1)
-            dve.wait_ge(S["z%d" % k], 4)
-            dve.wait_ge(S["s%d" % k], 1)
-            dve.tensor_tensor(T.hh[:, o:o + 2 * n], T.sl[:, o:o + 2 * n], ps[:, 2 * n:4 * n], mult).then_inc(S["h%d" % k], 1)
+        for i, k in enumerate(gr):
+            first_half(k)
+            if i:
+                second_half(gr[i - 1])
         if gi == 0:
             own_w2()
-        for k in gr:
-            n = TK * len(chunks[k])
-            ps = T["ps%d" % (2 + k)]
-            o = 2 * TK + k * 4 * TK
-            pe.wait_ge(S["h%d" % k], 1)
-            pe.matmul(ps[:, 4 * n:5 * n], T.wa[:, 2 * D:3 * D], T.hh[:, o:o + n], True, False).then_inc(S["p%d" % k], 1)
-            pe.matmul(ps[:, 4 * n:5 * n], T.wb[:, 2 * D:3 * D], T.hh[:, o + n:o + 2 * n], False, True).then_inc(S["p%d" % k], 1)
-            dve.wait_ge(S["p%d" % k], 2)
-            dve.tensor_copy(T.po[:, 2 * k * TK:2 * k * TK + n], ps[:, 4 * n:5 * n]).then_inc(S["c%d" % k], 1)
+        second_half(gr[-1])
 
     rets = P["rets"][core]
     dve.wait_ge(S.yp, 2)

from concourse.bass import DstId, RemoteDMATransfer
from concourse.mybir import AluOpType, ActivationFunctionType

TK = 32
D = 128
MAXCH = 4
NRET = 5
NHOP = 4

SCRATCH = {
    "xd": ("dram", [128, TK], "bfloat16"),
    "xh": ("dram", [128, TK], "bfloat16"),
    "xq": ("sbuf", [128, 2 * TK], "bfloat16"),
    "xo": ("sbuf", [128, TK], "bfloat16"),
    "xin": ("sbuf", [128, 2 * MAXCH * TK], "bfloat16"),
    "wa": ("sbuf", [128, 3 * D], "bfloat16"),
    "wb": ("sbuf", [128, 3 * D], "bfloat16"),
    "sl": ("sbuf", [128, 2 * TK + MAXCH * 4 * TK], "float32"),
    "hh": ("sbuf", [128, 2 * TK + MAXCH * 4 * TK], "bfloat16"),
    "po": ("sbuf", [128, 2 * MAXCH * TK], "bfloat16"),
    "land": ("sbuf", [128, NRET * TK], "bfloat16"),
    "acc": ("sbuf", [128, TK], "float32"),
    "ysb": ("sbuf", [128, TK], "bfloat16"),
}
for _i in range(2 + MAXCH):
    SCRATCH["ps%d" % _i] = ("psum", [128, 512], "float32")

SEMAPHORES = (["xl", "xm", "wl", "ws", "xg", "sent", "st", "yp", "ac"]
              + ["xs%d" % r for r in range(12)] + ["r%d" % q for q in range(NRET)]
              + ["%s%s" % (a, c) for a in "zsh" for c in ["A", "B"] + list(range(MAXCH))]
              + ["%s%d" % (a, c) for a in "pc" for c in range(MAXCH)])


def _bits(m):
    return [b for b in range(m.bit_length()) if (m >> b) & 1]


def _mask(bits):
    m = 0
    for b in bits:
        m |= 1 << b
    return m


def _plan(cores, topo):
    rk = {c: i for i, c in enumerate(cores)}
    chips = {}
    for c in cores:
        chips.setdefault((topo.host(c), topo.chip(c)), []).append(c)
    keys = list(chips)
    chip_of = {c: k for k in keys for c in chips[k]}
    planes = []
    for k in keys:
        for pl in planes:
            if topo.same_plane(chips[k][0], chips[pl[0]][0]):
                pl.append(k)
                break
        else:
            planes.append([k])
    reach = {c: sum(1 for d in cores if d != c and topo.may_write(c, d)) for c in cores}
    plain = {k: min(chips[k], key=lambda c: (reach[c], c)) for k in keys}
    port = {k: [c for c in chips[k] if c != plain[k]][0] for k in keys}
    sib = {c: [d for d in chips[chip_of[c]] if d != c][0] for c in cores}

    def handler(k, r):
        return min([h for h in chips[k] if topo.may_write(h, r)], key=lambda h: (reach[h], h))

    far_of, same_of = {}, {}
    for pl in planes:
        cross = [k for k in keys if k not in pl]
        for i, k in enumerate(pl):
            rot = i * len(cross) // len(pl) if len(pl) > len(cross) else 0
            far_of[k] = cross[rot:] + cross[:rot]
            same_of[k] = pl[i + 1:] + pl[:i]
    gath = {k: len(pl) < len(keys) - len(pl) for pl in planes for k in pl}
    cls, pos, wsem = {}, {}, {}
    for k in keys:
        for c in chips[k]:
            for j, k2 in enumerate(far_of[k] + same_of[k]):
                h = handler(k2, c)
                cls[(h, c)] = 0 if (c == port[k] or k2 in same_of[k]) else 2
                late_g = gath[k] and cls[(h, c)] == 2
                pos[(h, c)] = 0 if late_g else j
                wsem[(h, c)] = "xg" if late_g else "xs%d" % rk[c]
    src = {h: sorted([r for r in cores if (h, r) in cls], key=lambda r: (cls[(h, r)], pos[(h, r)], rk[r])) for h in cores}
    blk = {(h, r): src[h].index(r) for h in cores for r in src[h]}
    calls = {c: [] for c in cores}
    for pl in planes:
        pls = [plain[k] for k in pl]
        for i, k in enumerate(pl):
            a, b = plain[k], port[k]
            same = {c: [(handler(k2, c), "xin", blk[(handler(k2, c), c)], 1) for k2 in same_of[k]] for c in (a, b)}
            far = {c: [(handler(k2, c), "xin", blk[(handler(k2, c), c)], 1) for k2 in far_of[k]] for c in (a, b)}
            calls[b].append(([], "xd", far[b] + same[b], "xs%d" % rk[b], False))
            if gath[k]:
                calls[a].append(([], "xd", [(port[k2], "xq", i, 1) for k2 in same_of[k] + [k]], "xs%d" % rk[a], False))
                n = len(far_of[k]) // len(pl)
                mine = far_of[k][i * n:(i + 1) * n]
                calls[b].append((["xs%d" % rk[c] for c in pls], "xq",
                                 [(handler(k2, a), "xin", blk[(handler(k2, a), pls[0])], len(pls)) for k2 in mine], "xg", False))
            else:
                calls[a].append(([], "xd", [(b, "xh", None, 1)], "xs%d" % rk[a], True))
                calls[b].append((["xs%d" % rk[a]], "xh", far[a], "xs%d" % rk[a], False))
            calls[a].append(([], "xd", same[a], "xs%d" % rk[a], False))
    rets = {r: sorted([h for h in cores if (h, r) in cls], key=lambda h: (cls[(h, r)], blk[(h, r)], rk[h])) for r in cores}
    return {"sib": sib, "calls": calls, "src": src, "cls": cls, "wait": wsem, "rets": rets}


def rank_program(g, core, T, topo):
    if T.rank_of(core) is None:
        return
    cores = list(T.cores)
    P = _plan(cores, topo)
    S = T.sem
    sib = P["sib"][core]
    pe, act, dve, sy = g.tensor, g.scalar, g.vector, g.sync
    mult, add = AluOpType.mult, AluOpType.add
    silu = ActivationFunctionType.Silu

    far_mask = topo.mask(core, sib)
    for d in cores:
        if d != core and topo.may_write(core, d):
            far_mask &= topo.mask(core, d)
    near_mask = topo.mask(core, sib) & ~far_mask
    fb = _bits(far_mask)
    NF, NN = len(fb), len(_bits(near_mask))
    hop_mask = _mask(_bits(near_mask)[:NHOP])

    def cols(buf, b, n=1):
        return T[buf][:, b * TK:(b + n) * TK]

    def transfer(src, dests, sem, mask):
        ids = []
        for d, _ in dests:
            rid, pid = topo.addr(d, core)
            ids.append(DstId(rid=rid, pnc=pid))
        return RemoteDMATransfer(dst_ids=ids, dma_engine_mask=mask, remote_sem=sem, srcs=[src],
                                 dsts=[ap for _, ap in dests])

    xown = T.xo[:, :]
    src = P["src"][core]
    chunks = [src[i:i + 2] for i in range(0, len(src), 2)]
    late = [max(P["cls"][(core, r)] for r in ch) == 2 for ch in chunks]
    groups = [[k for k in range(len(chunks)) if late[k] == f] for f in (False, True)]
    groups = [gr for gr in groups if gr]

    sy.dma_start(T.xd[:, :], T.x[:, :]).then_inc(S.xl, 16)
    act.dma_start(T.wa[:, 0:D], T.w1[:, :]).then_inc(S.wl, 16)
    sy.dma_start(xown, T.x[:, :]).then_inc(S.xm, 16)
    act.dma_start(T.wa[:, D:2 * D], T.w3[:, :]).then_inc(S.wl, 16)
    sy.dma_start(T.wa[:, 2 * D:3 * D], T.w2[:, :]).then_inc(S.wl, 16)

    inc = {}
    for c in cores:
        for call in P["calls"][c]:
            for d, _, _, _ in call[2]:
                if d == core:
                    inc[call[3]] = NHOP if call[4] else NF

    sent = 0
    g.wait_ge(S.xl, 16)
    first_wait = [i for i, call in enumerate(P["calls"][core]) if call[0]]
    w_at = first_wait[0] if first_wait else len(P["calls"][core])

    def send_weights():
        rid, pid = topo.addr(sib, core)
        g.wait_ge(S.wl, 48)
        g.remote_dma(out_ap=T.wb[:, :], in_ap=T.wa[:, :], remote_sem=S.ws, local_sem=S.sent, pid=pid, routing_id=rid,
                     dma_engine_mask=near_mask)
        return NN

    for i, call in enumerate(P["calls"][core]):
        if i == w_at:
            sent += send_weights()
        waits, sbuf, dests, sem, hop = call
        for w in waits:
            g.wait_ge(S[w], inc[w])
        m = hop_mask if hop else far_mask
        g.remote_dma_fused([transfer(T[sbuf][:, :], [(d, T[buf][:, :] if b is None else cols(buf, b, n)) for d, buf, b, n in dests],
                                     S[sem], m)], local_sem=S.sent)
        sent += len(_bits(m))
    if w_at == len(P["calls"][core]):
        sent += send_weights()
    for k, ch in enumerate(chunks):
        g.wait_ge(S["c%d" % k], 1)
        ne = NF // len(ch)
        trs = []
        for j, r in enumerate(ch):
            q = P["rets"][r].index(core)
            trs.append(transfer(cols("po", 2 * k + j), [(r, cols("land", q))], S["r%d" % q],
                                _mask(fb[j * ne:(j + 1) * ne])))
            sent += ne
        g.remote_dma_fused(trs, local_sem=S.sent)
    g.wait_ge(S.sent, sent)

    W = {"A": T.wa, "B": T.wb}
    own_ps = {"A": T.ps0, "B": T.ps1}
    own_off = {"A": 0, "B": TK}

    pe.wait_ge(S.xm, 16)
    pe.wait_ge(S.wl, 48)
    for s in ("A", "B"):
        if s == "B":
            pe.wait_ge(S.ws, NN)
        ps, o = own_ps[s], own_off[s]
        pe.matmul(ps[:, 0:TK], W[s][:, 0:D], xown, True, True).then_inc(S["z" + s], 1)
        pe.matmul(ps[:, TK:2 * TK], W[s][:, D:2 * D], xown, True, True).then_inc(S["z" + s], 1)
        act.wait_ge(S["z" + s], 2)
        act.activation(T.sl[:, o:o + TK], ps[:, 0:TK], silu).then_inc(S["s" + s], 1)
        dve.wait_ge(S["z" + s], 2)
        dve.wait_ge(S["s" + s], 1)
        dve.tensor_tensor(T.hh[:, o:o + TK], T.sl[:, o:o + TK], ps[:, TK:2 * TK], mult).then_inc(S["h" + s], 1)

    yown = T.ps1[:, 2 * TK:3 * TK]

    def own_w2():
        pe.wait_ge(S.hA, 1)
        pe.wait_ge(S.hB, 1)
        pe.matmul(yown, T.wa[:, 2 * D:3 * D], T.hh[:, 0:TK], True, False).then_inc(S.yp, 1)
        pe.matmul(yown, T.wb[:, 2 * D:3 * D], T.hh[:, TK:2 * TK], False, True).then_inc(S.yp, 1)

    def first_half(k):
        n = TK * len(chunks[k])
        ps = T["ps%d" % (2 + k)]
        o = 2 * TK + k * 4 * TK
        xk = T.xin[:, 2 * k * TK:2 * k * TK + n]
        for w in sorted(set(P["wait"][(core, r)] for r in chunks[k])):
            pe.wait_ge(S[w], inc[w])
        pe.matmul(ps[:, 0:n], T.wa[:, 0:D], xk, True, True).then_inc(S["z%d" % k], 1)
        pe.matmul(ps[:, n:2 * n], T.wb[:, 0:D], xk, True, True).then_inc(S["z%d" % k], 1)
        pe.matmul(ps[:, 2 * n:3 * n], T.wa[:, D:2 * D], xk, True, True).then_inc(S["z%d" % k], 1)
        pe.matmul(ps[:, 3 * n:4 * n], T.wb[:, D:2 * D], xk, True, True).then_inc(S["z%d" % k], 1)
        act.wait_ge(S["z%d" % k], 4)
        act.activation(T.sl[:, o:o + 2 * n], ps[:, 0:2 * n], silu).then_inc(S["s%d" % k], 1)
        dve.wait_ge(S["z%d" % k], 4)
        dve.wait_ge(S["s%d" % k], 1)
        dve.tensor_tensor(T.hh[:, o:o + 2 * n], T.sl[:, o:o + 2 * n], ps[:, 2 * n:4 * n], mult).then_inc(S["h%d" % k], 1)

    def second_half(k):
        n = TK * len(chunks[k])
        ps = T["ps%d" % (2 + k)]
        o = 2 * TK + k * 4 * TK
        pe.wait_ge(S["h%d" % k], 1)
        pe.matmul(ps[:, 4 * n:5 * n], T.wa[:, 2 * D:3 * D], T.hh[:, o:o + n], True, False).then_inc(S["p%d" % k], 1)
        pe.matmul(ps[:, 4 * n:5 * n], T.wb[:, 2 * D:3 * D], T.hh[:, o + n:o + 2 * n], False, True).then_inc(S["p%d" % k], 1)
        dve.wait_ge(S["p%d" % k], 2)
        dve.tensor_copy(T.po[:, 2 * k * TK:2 * k * TK + n], ps[:, 4 * n:5 * n]).then_inc(S["c%d" % k], 1)

    for gi, gr in enumerate(groups):
        for i, k in enumerate(gr):
            first_half(k)
            if i:
                second_half(gr[i - 1])
        if gi == 0:
            own_w2()
        second_half(gr[-1])

    rets = P["rets"][core]
    dve.wait_ge(S.yp, 2)
    for q, h in enumerate(rets):
        hs = P["src"][h]
        hch = [hs[i:i + 2] for i in range(0, len(hs), 2) if core in hs[i:i + 2]][0]
        dve.wait_ge(S["r%d" % q], NF // len(hch))
        if q:
            dve.wait_ge(S.ac, q)
        dve.tensor_tensor(T.ysb[:, :] if q == len(rets) - 1 else T.acc[:, :], yown if q == 0 else T.acc[:, :],
                          cols("land", q), add).then_inc(S.ac, 1)
    sy.wait_ge(S.ac, len(rets))
    sy.dma_start(T.y[:, :], T.ysb[:, :]).then_inc(S.st, 16)
    sy.wait_ge(S.st, 16)
